import numpy as np
import ml_dtypes


def mxq(x, axis, fmt="e4m3"):
    dtype, down = {"e4m3": (ml_dtypes.float8_e4m3fn, 7), "e5m2": (ml_dtypes.float8_e5m2, 14)}[fmt]
    v = np.moveaxis(np.asarray(x, np.float32).astype(ml_dtypes.bfloat16).astype(np.float64), axis, -1)
    blocks = v.reshape(v.shape[:-1] + (-1, 32))
    amax = np.abs(blocks).max(-1, keepdims=True)
    byte = np.maximum(np.where(amax > 0, np.frexp(amax)[1] - 1 + 127, 0) - down, 1)
    scale = np.exp2(byte - 127.0)
    codes = (blocks / scale).astype(np.float32).astype(dtype).astype(np.float64)
    return np.moveaxis((codes * scale).reshape(v.shape), -1, axis)


WIDE = False


def mx_kscale(k):
    if not WIDE:
        return np.ones(k)
    levels = np.array([10, -10, 5, -5, 0])
    if k % 512:
        return np.exp2(np.random.permutation(np.resize(levels, k // 32))).repeat(32)
    a = np.empty((k // 512, 16))
    for p in range(k // 512):
        a[p, :8] = np.random.permutation(np.resize(levels, 8))
        for g in range(8):
            far = levels[np.abs(levels - a[p, g]) >= 10]
            a[p, g + 8] = far[np.random.randint(len(far))]
    return np.exp2(a.ravel()).repeat(32)


def f64(x):
    return np.asarray(x).astype(np.float64)


def striped(idx):
    return np.tile(np.asarray(idx).reshape(-1, 16).T, (8, 1)).astype(np.uint16)


def unstriped(offs):
    return offs[:16].T.reshape(-1).astype(np.int64)


E2M1 = np.array([0.0, 0.5, 1.0, 1.5, 2.0, 3.0, 4.0, 6.0, -0.0, -0.5, -1.0, -1.5, -2.0, -3.0, -4.0, -6.0])


def pack_weight(w, fmt):
    k, n = w.shape
    w = f64(np.asarray(w, np.float32).astype(ml_dtypes.bfloat16)).reshape(k // 32, 32, n)
    amax = np.abs(w).max(1)
    if fmt == "e4m3":
        byte = np.frexp(amax)[1] - 1 + 127 - 7
    else:
        mant, ex = np.frexp(amax / 6.0)
        byte = np.where(mant > 0.5, ex, ex - 1) + 127
    byte = np.clip(np.where(amax > 0, byte, 1), 1, 254)
    scaled = (w * np.exp2(127.0 - byte)[:, None, :]).reshape(k, n).astype(np.float32)
    by_word = np.ascontiguousarray(scaled.reshape(k // 512, 128, 4, n).transpose(0, 1, 3, 2))
    if fmt == "e4m3":
        words = by_word.astype(ml_dtypes.float8_e4m3fn).view(np.uint8)
    else:
        c = by_word.astype(ml_dtypes.float4_e2m1fn).view(np.uint8) & 0xF
        words = (c[..., 0::2] | (c[..., 1::2] << 4)).reshape(k // 512, 128, 2 * n)
    return np.ascontiguousarray(words), np.ascontiguousarray(byte.astype(np.uint8).reshape(k // 512, 16, n))


def unpack_weight(words, scales, fmt):
    g, _, n = scales.shape
    words = np.ascontiguousarray(words).reshape(g, 128, n, -1)
    if fmt == "e4m3":
        vals = words.view(ml_dtypes.float8_e4m3fn).astype(np.float64)
    else:
        nib = np.empty((g, 128, n, 4), np.uint8)
        nib[..., 0::2] = words & 0xF
        nib[..., 1::2] = words >> 4
        vals = E2M1[nib]
    vals = vals * np.repeat(np.exp2(scales.astype(np.float64) - 127.0), 8, axis=1)[..., None]
    return vals.transpose(0, 1, 3, 2).reshape(g * 512, n)


def sigmoid(v):
    return 1.0 / (1.0 + np.exp(-v))


K, L, T, C, J = 512, 512, 512, 1024, 512


def setup_inputs():
    n = np.random.standard_normal
    idx = np.random.permutation(C)[:J]
    idx2 = np.random.permutation(C)[:J]
    fk = mx_kscale(K)
    fl = mx_kscale(L)
    xtp = pack_weight(n((K, T)) / fk[:, None], "e4m3")
    xsp = pack_weight(n((L, T)) / fl[:, None], "e2m1")
    wsp = pack_weight(n((L, J)) * 1 / np.sqrt(L) * fl[:, None], "e4m3")
    return {
        "xt_words": xtp[0],
        "xt_scales": xtp[1],
        "wc": (n((K, C)) * 1 / np.sqrt(K) * fk[:, None]).astype(np.float32),
        "xs_words": xsp[0],
        "xs_scales": xsp[1],
        "ws_words": wsp[0],
        "ws_scales": wsp[1],
        "offs": striped(idx),
        "offs2": striped(idx2),
    }


def reference(xt_words, xt_scales, wc, xs_words, xs_scales, ws_words, ws_scales, offs, offs2):
    idx = unstriped(offs)
    idx2 = unstriped(offs2)
    xtu = unpack_weight(xt_words, xt_scales, "e4m3")
    xsu = unpack_weight(xs_words, xs_scales, "e2m1")
    wsu = unpack_weight(ws_words, ws_scales, "e4m3")
    wcq = mxq(f64(wc), 0, "e4m3")
    z = xtu.T @ wcq
    s = xsu.T @ wsu
    y = z[:, idx] * sigmoid(z[:, idx2]) * s
    return y

@@ -1,0 +1,162 @@
+from contextlib import ExitStack
+
+import concourse.mybir as mybir
+
+K, L, T, C, J = 512, 512, 512, 1024, 512
+FLOPS = 2 * K * T * C + 2 * L * T * J
+
+F32 = mybir.dt.float32
+BF16 = mybir.dt.bfloat16
+I32 = mybir.dt.int32
+U32 = mybir.dt.uint32
+U16 = mybir.dt.uint16
+U8 = mybir.dt.uint8
+FP8X4 = mybir.dt.float8_e4m3fn_x4
+FP4X4 = mybir.dt.float4_e2m1fn_x4
+MULT = mybir.AluOpType.mult
+SIGMOID = mybir.ActivationFunctionType.Sigmoid
+
+P = 128
+PACK = 4
+TILES = T // P
+BANK = 512
+CHUNKS = (256, 256, 256, 128, 128)
+
+
+def load_scale_rows(queue, plane, scales):
+    for q in range(4):
+        queue.dma_start(plane[32 * q : 32 * q + 4, :].bitcast(I32), scales[0, 4 * q : 4 * q + 4, :].bitcast(I32))
+
+
+def load_scale_quadrants(queue, plane, scales):
+    for q in range(4):
+        rows = scales[0, 4 * q : 4 * q + 4, :].bitcast(I32)
+        queue.dma_start(plane[32 * q : 32 * q + 32, :].bitcast(I32), rows.unsqueeze(0).to_broadcast([8, 4, rows.shape[1]]))
+
+
+def tile_list_two_pickers_one_row_kernel(tc, xt_words, xt_scales, wc, xs_words, xs_scales, ws_words, ws_scales, offs, offs2, out):
+    nc = tc.nc
+    with ExitStack() as ctx:
+        keep = ctx.enter_context(tc.tile_pool(name="keep", bufs=1))
+        psum = ctx.enter_context(tc.psum_pool(name="psum", bufs=1))
+
+        xt_plane = keep.tile([P, T], U8, name="xt_plane", align_bytes=64)
+        xs_plane = keep.tile([P, T], U8, name="xs_plane", align_bytes=64)
+        ws_plane = keep.tile([P, J], U8, name="ws_plane", align_bytes=64)
+        for plane in (xs_plane, ws_plane):
+            nc.gpsimd.memset(plane[:].bitcast(I32), 0)
+
+        warm_in = keep.tile([P, 8], F32, name="warm_in")
+        warm_out = keep.tile([P, 8], F32, name="warm_out")
+        nc.vector.memset(warm_in[:], 0.0)
+        nc.scalar.activation(warm_out[:], warm_in[:], SIGMOID)
+
+        starts = [sum(CHUNKS[:i]) for i in range(len(CHUNKS))]
+        wc_rows = wc.rearrange("(p r) c -> p r c", r=PACK)
+        raw = [keep.tile([P, PACK, w], F32, name=f"raw{i}", align_bytes=64) for i, w in enumerate(CHUNKS)]
+
+        def load_chunk(i):
+            nc.sync.dma_start(raw[i][:], wc_rows[:, :, starts[i] : starts[i] + CHUNKS[i]])
+
+        xt_codes = keep.tile([P, T], U32, name="xt_codes", align_bytes=64)
+        xs_codes = keep.tile([P, 2 * T], U8, name="xs_codes", align_bytes=64)
+        ws_codes = keep.tile([P, J], U32, name="ws_codes", align_bytes=64)
+        value_list = keep.tile([P, J // 16], U16, name="value_list")
+        gate_list = keep.tile([P, J // 16], U16, name="gate_list")
+
+        load_scale_rows(nc.gpsimd, xs_plane, xs_scales)
+        load_chunk(0)
+        nc.sync.dma_start(xt_codes[:].bitcast(I32), xt_words[0].rearrange("p n r -> p (n r)").bitcast(I32))
+        load_scale_quadrants(nc.sync, xt_plane, xt_scales)
+        load_chunk(1)
+        load_chunk(2)
+        load_chunk(3)
+        load_chunk(4)
+        load_scale_rows(nc.sync, ws_plane, ws_scales)
+        nc.sync.dma_start(ws_codes[:].bitcast(I32), ws_words[0].rearrange("p n r -> p (n r)").bitcast(I32))
+        nc.sync.dma_start(xs_codes[:].bitcast(I32), xs_words[0].bitcast(I32))
+        nc.sync.dma_start(gate_list[:], offs2)
+        nc.sync.dma_start(value_list[:], offs)
+
+        z = [keep.tile([P, C], F32, name=f"z{m}") for m in range(TILES)]
+        wc_codes = []
+        wc_planes = []
+
+        def quantise(i):
+            w = CHUNKS[i]
+            grouped = keep.tile([P, w, PACK], BF16, name=f"grouped{i}", align_bytes=64)
+            nc.vector.tensor_copy(
+                grouped[:].rearrange("p (c i) r -> p c r i", i=4),
+                raw[i][:].rearrange("p r (c i) -> p c r i", i=4),
+            )
+            codes = keep.tile([P, w], U32, name=f"wc_codes{i}", align_bytes=64)
+            plane = keep.tile([P, w], U8, name=f"wc_plane{i}", align_bytes=64)
+            nc.vector.quantize_mx(out=codes[:].bitcast(FP8X4), scales=plane[:], in_=grouped[:].rearrange("p c r -> p (c r)"))
+            wc_codes.append(codes)
+            wc_planes.append(plane)
+
+        def z_product(i, m, bank_cols):
+            cols = slice(m * P, (m + 1) * P)
+            nc.tensor.matmul_mx(
+                out=bank_cols, lhsT=xt_codes[:, cols].bitcast(FP8X4), lhsT_scale=xt_plane[:, cols],
+                rhs=wc_codes[i][:].bitcast(FP8X4), rhs_scale=wc_planes[i][:], start=True, stop=True)
+
+        def bank_tile(name, width, n):
+            return psum.tile([P, width], F32, name=name, tag=f"bank{n}")
+
+        for i in range(2):
+            quantise(i)
+            for m in range(TILES):
+                bank = bank_tile(f"zbank{i}_{m}", CHUNKS[i], i * TILES + m)
+                z_product(i, m, bank[:])
+                nc.scalar.copy(z[m][:, starts[i] : starts[i] + CHUNKS[i]], bank[:])
+        quantise(2)
+        third = []
+        for m in range(TILES):
+            third.append(bank_tile(f"zbank2_{m}", CHUNKS[2], m))
+            z_product(2, m, third[m][:])
+        fourth = []
+        quantise(3)
+        for m in range(TILES):
+            fourth.append(bank_tile(f"zbank3_{m}", CHUNKS[3] + CHUNKS[4], TILES + m))
+            z_product(3, m, fourth[m][:, 0 : CHUNKS[3]])
+        quantise(4)
+        for m in range(TILES):
+            z_product(4, m, fourth[m][:, CHUNKS[3] :])
+
+        def finish_z(m, last_copy):
+            nc.scalar.copy(z[m][:, starts[2] : starts[3]], third[m][:])
+            last_copy(z[m][:, starts[3] :], fourth[m][:])
+
+        def s_product(m):
+            s_bank = bank_tile(f"sbank{m}", J, m)
+            nc.tensor.matmul_mx(
+                out=s_bank[:], lhsT=xs_codes[:, 2 * m * P : 2 * (m + 1) * P].bitcast(FP4X4), lhsT_scale=xs_plane[:, m * P : (m + 1) * P],
+                rhs=ws_codes[:].bitcast(FP8X4), rhs_scale=ws_plane[:], start=True, stop=True)
+            return s_bank
+
+        finish_z(0, nc.scalar.copy)
+        finish_z(1, nc.vector.tensor_copy)
+        for m in range(TILES):
+            if m >= 2:
+                finish_z(m, nc.scalar.copy)
+            s_bank = s_product(m)
+            gate = keep.tile([P, J], F32, name=f"gate{m}")
+            nc.scalar.activation(gate[:], z[m][:].indirect(gate_list[:]), SIGMOID)
+            factor = keep.tile([P, J], F32, name=f"factor{m}")
+            result = keep.tile([P, J], F32, name=f"result{m}")
+            rows = out[m * P : (m + 1) * P, :]
+            if m == 0:
+                value = keep.tile([P, J], F32, name="value")
+                nc.vector.tensor_copy(value[:], z[m][:].indirect(value_list[:]))
+                nc.vector.tensor_tensor(factor[:], value[:], gate[:], MULT)
+                nc.vector.tensor_tensor(result[:], factor[:], s_bank[:], MULT)
+                nc.sync.dma_start(rows, result[:])
+            else:
+                parts = 2 if m == TILES - 1 else 1
+                nc.vector.tensor_tensor(factor[:], gate[:], s_bank[:], MULT)
+                for h in range(parts):
+                    cols = slice(h * J // parts, (h + 1) * J // parts)
+                    picks = value_list[:, h * J // parts // 16 : (h + 1) * J // parts // 16]
+                    nc.vector.tensor_tensor(result[:, cols], z[m][:].indirect(picks), factor[:, cols], MULT)
+                    nc.sync.dma_start(rows[:, cols], result[:, cols])

@@ -20,18 +20,14 @@ P = 128
 PACK = 4
 TILES = T // P
 BANK = 512
+LOADS = (256, 256, 256, 256)
 CHUNKS = (256, 256, 256, 128, 128)
+LOAD_OF = (0, 1, 2, 3, 3)
 
 
 def load_scale_rows(queue, plane, scales):
     for q in range(4):
         queue.dma_start(plane[32 * q : 32 * q + 4, :].bitcast(I32), scales[0, 4 * q : 4 * q + 4, :].bitcast(I32))
-
-
-def load_scale_quadrants(queue, plane, scales):
-    for q in range(4):
-        rows = scales[0, 4 * q : 4 * q + 4, :].bitcast(I32)
-        queue.dma_start(plane[32 * q : 32 * q + 32, :].bitcast(I32), rows.unsqueeze(0).to_broadcast([8, 4, rows.shape[1]]))
 
 
 def tile_list_two_pickers_one_row_kernel(tc, xt_words, xt_scales, wc, xs_words, xs_scales, ws_words, ws_scales, offs, offs2, out):
@@ -43,8 +39,9 @@ def tile_list_two_pickers_one_row_kernel(tc, xt_words, xt_scales, wc, xs_words, 
         xt_plane = keep.tile([P, T], U8, name="xt_plane", align_bytes=64)
         xs_plane = keep.tile([P, T], U8, name="xs_plane", align_bytes=64)
         ws_plane = keep.tile([P, J], U8, name="ws_plane", align_bytes=64)
-        for plane in (xs_plane, ws_plane):
-            nc.gpsimd.memset(plane[:].bitcast(I32), 0)
+        nc.vector.memset(xt_plane[:].bitcast(I32), 0)
+        nc.vector.memset(ws_plane[:].bitcast(I32), 0)
+        nc.gpsimd.memset(xs_plane[:].bitcast(I32), 0)
 
         warm_in = keep.tile([P, 8], F32, name="warm_in")
         warm_out = keep.tile([P, 8], F32, name="warm_out")
@@ -53,10 +50,11 @@ def tile_list_two_pickers_one_row_kernel(tc, xt_words, xt_scales, wc, xs_words, 
 
         starts = [sum(CHUNKS[:i]) for i in range(len(CHUNKS))]
         wc_rows = wc.rearrange("(p r) c -> p r c", r=PACK)
-        raw = [keep.tile([P, PACK, w], F32, name=f"raw{i}", align_bytes=64) for i, w in enumerate(CHUNKS)]
+        load_starts = [sum(LOADS[:i]) for i in range(len(LOADS))]
+        raw = [keep.tile([P, PACK, w], F32, name=f"raw{i}", align_bytes=64) for i, w in enumerate(LOADS)]
 
         def load_chunk(i):
-            nc.sync.dma_start(raw[i][:], wc_rows[:, :, starts[i] : starts[i] + CHUNKS[i]])
+            nc.sync.dma_start(raw[i][:], wc_rows[:, :, load_starts[i] : load_starts[i] + LOADS[i]])
 
         xt_codes = keep.tile([P, T], U32, name="xt_codes", align_bytes=64)
         xs_codes = keep.tile([P, 2 * T], U8, name="xs_codes", align_bytes=64)
@@ -67,33 +65,30 @@ def tile_list_two_pickers_one_row_kernel(tc, xt_words, xt_scales, wc, xs_words, 
         load_scale_rows(nc.gpsimd, xs_plane, xs_scales)
         load_chunk(0)
         nc.sync.dma_start(xt_codes[:].bitcast(I32), xt_words[0].rearrange("p n r -> p (n r)").bitcast(I32))
-        load_scale_quadrants(nc.sync, xt_plane, xt_scales)
+        load_scale_rows(nc.sync, xt_plane, xt_scales)
         load_chunk(1)
         load_chunk(2)
         load_chunk(3)
-        load_chunk(4)
-        load_scale_rows(nc.sync, ws_plane, ws_scales)
+        nc.sync.dma_start(gate_list[:], offs2)
         nc.sync.dma_start(ws_codes[:].bitcast(I32), ws_words[0].rearrange("p n r -> p (n r)").bitcast(I32))
         nc.sync.dma_start(xs_codes[:].bitcast(I32), xs_words[0].bitcast(I32))
-        nc.sync.dma_start(gate_list[:], offs2)
+        load_scale_rows(nc.sync, ws_plane, ws_scales)
         nc.sync.dma_start(value_list[:], offs)
 
         z = [keep.tile([P, C], F32, name=f"z{m}") for m in range(TILES)]
-        wc_codes = []
-        wc_planes = []
+        grouped = [keep.tile([P, w, PACK], BF16, name=f"grouped{i}", align_bytes=64) for i, w in enumerate(CHUNKS)]
+        wc_codes = [keep.tile([P, w], U32, name=f"wc_codes{i}", align_bytes=64) for i, w in enumerate(CHUNKS)]
+        wc_planes = [keep.tile([P, w], U8, name=f"wc_plane{i}", align_bytes=64) for i, w in enumerate(CHUNKS)]
+
+        def interleave(i, copy):
+            first = starts[i] - load_starts[LOAD_OF[i]]
+            copy(
+                grouped[i][:].rearrange("p (c i) r -> p c r i", i=4),
+                raw[LOAD_OF[i]][:, :, first : first + CHUNKS[i]].rearrange("p r (c i) -> p c r i", i=4),
+            )
 
         def quantise(i):
-            w = CHUNKS[i]
-            grouped = keep.tile([P, w, PACK], BF16, name=f"grouped{i}", align_bytes=64)
-            nc.vector.tensor_copy(
-                grouped[:].rearrange("p (c i) r -> p c r i", i=4),
-                raw[i][:].rearrange("p r (c i) -> p c r i", i=4),
-            )
-            codes = keep.tile([P, w], U32, name=f"wc_codes{i}", align_bytes=64)
-            plane = keep.tile([P, w], U8, name=f"wc_plane{i}", align_bytes=64)
-            nc.vector.quantize_mx(out=codes[:].bitcast(FP8X4), scales=plane[:], in_=grouped[:].rearrange("p c r -> p (c r)"))
-            wc_codes.append(codes)
-            wc_planes.append(plane)
+            nc.vector.quantize_mx(out=wc_codes[i][:].bitcast(FP8X4), scales=wc_planes[i][:], in_=grouped[i][:].rearrange("p c r -> p (c r)"))
 
         def z_product(i, m, bank_cols):
             cols = slice(m * P, (m + 1) * P)
@@ -104,29 +99,19 @@ def tile_list_two_pickers_one_row_kernel(tc, xt_words, xt_scales, wc, xs_words, 
         def bank_tile(name, width, n):
             return psum.tile([P, width], F32, name=name, tag=f"bank{n}")
 
-        for i in range(2):
-            quantise(i)
-            for m in range(TILES):
-                bank = bank_tile(f"zbank{i}_{m}", CHUNKS[i], i * TILES + m)
-                z_product(i, m, bank[:])
-                nc.scalar.copy(z[m][:, starts[i] : starts[i] + CHUNKS[i]], bank[:])
-        quantise(2)
-        third = []
-        for m in range(TILES):
-            third.append(bank_tile(f"zbank2_{m}", CHUNKS[2], m))
-            z_product(2, m, third[m][:])
-        fourth = []
-        quantise(3)
-        for m in range(TILES):
-            fourth.append(bank_tile(f"zbank3_{m}", CHUNKS[3] + CHUNKS[4], TILES + m))
-            z_product(3, m, fourth[m][:, 0 : CHUNKS[3]])
-        quantise(4)
-        for m in range(TILES):
-            z_product(4, m, fourth[m][:, CHUNKS[3] :])
+        banks = {}
 
-        def finish_z(m, last_copy):
-            nc.scalar.copy(z[m][:, starts[2] : starts[3]], third[m][:])
-            last_copy(z[m][:, starts[3] :], fourth[m][:])
+        def products(group, pieces, tiles):
+            for m in tiles:
+                width = sum(CHUNKS[i] for i in pieces)
+                banks[group, m] = bank_tile(f"zbank{group}_{m}", width, (group % 2) * TILES + m)
+                for i in pieces:
+                    first = starts[i] - starts[pieces[0]]
+                    z_product(i, m, banks[group, m][:, first : first + CHUNKS[i]])
+
+        def empty(group, m, copy):
+            bank = banks[group, m]
+            copy(z[m][:, starts[group] : starts[group] + bank.shape[1]], bank[:])
 
         def s_product(m):
             s_bank = bank_tile(f"sbank{m}", J, m)
@@ -135,28 +120,35 @@ def tile_list_two_pickers_one_row_kernel(tc, xt_words, xt_scales, wc, xs_words, 
                 rhs=ws_codes[:].bitcast(FP8X4), rhs_scale=ws_plane[:], start=True, stop=True)
             return s_bank
 
-        finish_z(0, nc.scalar.copy)
-        finish_z(1, nc.vector.tensor_copy)
-        for m in range(TILES):
-            if m >= 2:
-                finish_z(m, nc.scalar.copy)
-            s_bank = s_product(m)
+        def pick(m, s_bank):
             gate = keep.tile([P, J], F32, name=f"gate{m}")
-            nc.scalar.activation(gate[:], z[m][:].indirect(gate_list[:]), SIGMOID)
             factor = keep.tile([P, J], F32, name=f"factor{m}")
             result = keep.tile([P, J], F32, name=f"result{m}")
             rows = out[m * P : (m + 1) * P, :]
-            if m == 0:
-                value = keep.tile([P, J], F32, name="value")
-                nc.vector.tensor_copy(value[:], z[m][:].indirect(value_list[:]))
-                nc.vector.tensor_tensor(factor[:], value[:], gate[:], MULT)
-                nc.vector.tensor_tensor(result[:], factor[:], s_bank[:], MULT)
-                nc.sync.dma_start(rows, result[:])
-            else:
-                parts = 2 if m == TILES - 1 else 1
-                nc.vector.tensor_tensor(factor[:], gate[:], s_bank[:], MULT)
-                for h in range(parts):
-                    cols = slice(h * J // parts, (h + 1) * J // parts)
-                    picks = value_list[:, h * J // parts // 16 : (h + 1) * J // parts // 16]
-                    nc.vector.tensor_tensor(result[:, cols], z[m][:].indirect(picks), factor[:, cols], MULT)
-                    nc.sync.dma_start(rows[:, cols], result[:, cols])
+            halves = [(slice(h * J // 2, (h + 1) * J // 2), slice(h * J // 32, (h + 1) * J // 32)) for h in range(2)]
+            whole = [(slice(0, J), slice(0, J // 16))]
+            for cols, entries in halves if m == 0 else whole:
+                nc.scalar.activation(gate[:, cols], z[m][:].indirect(gate_list[:, entries]), SIGMOID)
+            for cols, entries in halves:
+                nc.vector.tensor_tensor(factor[:, cols], gate[:, cols], s_bank[:, cols], MULT)
+            for cols, entries in halves:
+                nc.vector.tensor_tensor(result[:, cols], z[m][:].indirect(value_list[:, entries]), factor[:, cols], MULT)
+            for cols, entries in halves if m == TILES - 1 else whole:
+                nc.sync.dma_start(rows[:, cols], result[:, cols])
+
+        for i in range(3):
+            interleave(i, nc.vector.tensor_copy)
+            quantise(i)
+            products(i, (i,), range(TILES))
+            for m in range(TILES):
+                empty(i, m, nc.scalar.copy)
+        interleave(3, nc.vector.tensor_copy)
+        interleave(4, nc.vector.tensor_copy)
+        quantise(3)
+        quantise(4)
+        products(3, (3, 4), range(TILES))
+        empty(3, 0, nc.scalar.copy)
+        for m in range(1, TILES):
+            empty(3, m, nc.vector.tensor_copy)
+        for m in range(TILES):
+            pick(m, s_product(m))

@@ -69,11 +69,11 @@ def tile_list_two_pickers_one_row_kernel(tc, xt_words, xt_scales, wc, xs_words, 
         load_chunk(1)
         load_chunk(2)
         load_chunk(3)
+        nc.sync.dma_start(value_list[:], offs)
         nc.sync.dma_start(gate_list[:], offs2)
         nc.sync.dma_start(ws_codes[:].bitcast(I32), ws_words[0].rearrange("p n r -> p (n r)").bitcast(I32))
         nc.sync.dma_start(xs_codes[:].bitcast(I32), xs_words[0].bitcast(I32))
         load_scale_rows(nc.sync, ws_plane, ws_scales)
-        nc.sync.dma_start(value_list[:], offs)
 
         z = [keep.tile([P, C], F32, name=f"z{m}") for m in range(TILES)]
         grouped = [keep.tile([P, w, PACK], BF16, name=f"grouped{i}", align_bytes=64) for i, w in enumerate(CHUNKS)]
@@ -99,56 +99,71 @@ def tile_list_two_pickers_one_row_kernel(tc, xt_words, xt_scales, wc, xs_words, 
         def bank_tile(name, width, n):
             return psum.tile([P, width], F32, name=name, tag=f"bank{n}")
 
-        banks = {}
+        def products(pieces, m, bank_cols):
+            for i in pieces:
+                first = starts[i] - starts[pieces[0]]
+                z_product(i, m, bank_cols[:, first : first + CHUNKS[i]])
 
-        def products(group, pieces, tiles):
-            for m in tiles:
-                width = sum(CHUNKS[i] for i in pieces)
-                banks[group, m] = bank_tile(f"zbank{group}_{m}", width, (group % 2) * TILES + m)
-                for i in pieces:
-                    first = starts[i] - starts[pieces[0]]
-                    z_product(i, m, banks[group, m][:, first : first + CHUNKS[i]])
-
-        def empty(group, m, copy):
-            bank = banks[group, m]
-            copy(z[m][:, starts[group] : starts[group] + bank.shape[1]], bank[:])
-
-        def s_product(m):
-            s_bank = bank_tile(f"sbank{m}", J, m)
+        def s_product(m, n):
+            s_bank = bank_tile(f"sbank{m}", J, n)
             nc.tensor.matmul_mx(
                 out=s_bank[:], lhsT=xs_codes[:, 2 * m * P : 2 * (m + 1) * P].bitcast(FP4X4), lhsT_scale=xs_plane[:, m * P : (m + 1) * P],
                 rhs=ws_codes[:].bitcast(FP8X4), rhs_scale=ws_plane[:], start=True, stop=True)
             return s_bank
+
+        def parts(*edges):
+            return [(slice(a, b), slice(a // 16, b // 16)) for a, b in zip(edges, edges[1:])]
+
+        whole, halves = parts(0, J), parts(0, J // 2, J)
 
         def pick(m, s_bank):
             gate = keep.tile([P, J], F32, name=f"gate{m}")
             factor = keep.tile([P, J], F32, name=f"factor{m}")
             result = keep.tile([P, J], F32, name=f"result{m}")
             rows = out[m * P : (m + 1) * P, :]
-            halves = [(slice(h * J // 2, (h + 1) * J // 2), slice(h * J // 32, (h + 1) * J // 32)) for h in range(2)]
-            whole = [(slice(0, J), slice(0, J // 16))]
-            for cols, entries in halves if m == 0 else whole:
+            for cols, entries in halves if m in (1, 2) else whole:
                 nc.scalar.activation(gate[:, cols], z[m][:].indirect(gate_list[:, entries]), SIGMOID)
+            if m == 0:
+                value = keep.tile([P, J], F32, name="value")
+                for cols, entries in halves:
+                    nc.vector.tensor_copy(value[:, cols], z[m][:].indirect(value_list[:, entries]))
+                for cols, entries in halves:
+                    nc.vector.tensor_tensor(factor[:, cols], value[:, cols], s_bank[:, cols], MULT)
+                for cols, entries in halves:
+                    nc.vector.tensor_tensor(result[:, cols], factor[:, cols], gate[:, cols], MULT)
+                nc.sync.dma_start(rows, result[:])
+                return
             for cols, entries in halves:
                 nc.vector.tensor_tensor(factor[:, cols], gate[:, cols], s_bank[:, cols], MULT)
-            for cols, entries in halves:
+            for cols, entries in halves if m < TILES - 1 else parts(0, J // 2, 3 * J // 4, J):
                 nc.vector.tensor_tensor(result[:, cols], z[m][:].indirect(value_list[:, entries]), factor[:, cols], MULT)
-            for cols, entries in halves if m == TILES - 1 else whole:
-                nc.sync.dma_start(rows[:, cols], result[:, cols])
+                if m == TILES - 1:
+                    nc.sync.dma_start(rows[:, cols], result[:, cols])
+            if m < TILES - 1:
+                nc.sync.dma_start(rows, result[:])
 
         for i in range(3):
             interleave(i, nc.vector.tensor_copy)
             quantise(i)
-            products(i, (i,), range(TILES))
             for m in range(TILES):
-                empty(i, m, nc.scalar.copy)
+                bank = bank_tile(f"zbank{i}_{m}", CHUNKS[i], (i % 2) * TILES + m)
+                products((i,), m, bank[:])
+                nc.scalar.copy(z[m][:, starts[i] : starts[i + 1]], bank[:])
         interleave(3, nc.vector.tensor_copy)
         interleave(4, nc.vector.tensor_copy)
         quantise(3)
         quantise(4)
-        products(3, (3, 4), range(TILES))
-        empty(3, 0, nc.scalar.copy)
-        for m in range(1, TILES):
-            empty(3, m, nc.vector.tensor_copy)
-        for m in range(TILES):
-            pick(m, s_product(m))
+        width = C - starts[3]
+        for m, copy in ((0, nc.scalar.copy), (1, nc.vector.tensor_copy)):
+            bank = bank_tile(f"zbank3_{m}", width, TILES + m)
+            products((3, 4), m, bank[:])
+            copy(z[m][:, starts[3] :], bank[:])
+        for m in range(2):
+            pick(m, s_product(m, m))
+        bank = bank_tile("zbank3_late", 2 * width, 0)
+        for m in range(2, TILES):
+            products((3, 4), m, bank[:, (m - 2) * width : (m - 1) * width])
+        for m in range(2, TILES):
+            nc.scalar.copy(z[m][:, starts[3] :], bank[:, (m - 2) * width : (m - 1) * width])
+        for m in range(2, TILES):
+            pick(m, s_product(m, m))

from contextlib import ExitStack

import concourse.mybir as mybir

K, L, T, C, J = 512, 512, 512, 1024, 512
FLOPS = 2 * K * T * C + 2 * L * T * J

F32 = mybir.dt.float32
BF16 = mybir.dt.bfloat16
I32 = mybir.dt.int32
U32 = mybir.dt.uint32
U16 = mybir.dt.uint16
U8 = mybir.dt.uint8
FP8X4 = mybir.dt.float8_e4m3fn_x4
FP4X4 = mybir.dt.float4_e2m1fn_x4
MULT = mybir.AluOpType.mult
SIGMOID = mybir.ActivationFunctionType.Sigmoid

P = 128
PACK = 4
TILES = T // P
BANK = 512
LOADS = (256, 256, 256, 256)
CHUNKS = (256, 256, 256, 128, 128)
LOAD_OF = (0, 1, 2, 3, 3)


def load_scale_rows(queue, plane, scales):
    for q in range(4):
        queue.dma_start(plane[32 * q : 32 * q + 4, :].bitcast(I32), scales[0, 4 * q : 4 * q + 4, :].bitcast(I32))


def tile_list_two_pickers_one_row_kernel(tc, xt_words, xt_scales, wc, xs_words, xs_scales, ws_words, ws_scales, offs, offs2, out):
    nc = tc.nc
    with ExitStack() as ctx:
        keep = ctx.enter_context(tc.tile_pool(name="keep", bufs=1))
        psum = ctx.enter_context(tc.psum_pool(name="psum", bufs=1))

        xt_plane = keep.tile([P, T], U8, name="xt_plane", align_bytes=64)
        xs_plane = keep.tile([P, T], U8, name="xs_plane", align_bytes=64)
        ws_plane = keep.tile([P, J], U8, name="ws_plane", align_bytes=64)
        nc.vector.memset(xt_plane[:].bitcast(I32), 0)
        nc.vector.memset(ws_plane[:].bitcast(I32), 0)
        nc.gpsimd.memset(xs_plane[:].bitcast(I32), 0)

        warm_in = keep.tile([P, 8], F32, name="warm_in")
        warm_out = keep.tile([P, 8], F32, name="warm_out")
        nc.vector.memset(warm_in[:], 0.0)
        nc.scalar.activation(warm_out[:], warm_in[:], SIGMOID)

        starts = [sum(CHUNKS[:i]) for i in range(len(CHUNKS))]
        wc_rows = wc.rearrange("(p r) c -> p r c", r=PACK)
        load_starts = [sum(LOADS[:i]) for i in range(len(LOADS))]
        raw = [keep.tile([P, PACK, w], F32, name=f"raw{i}", align_bytes=64) for i, w in enumerate(LOADS)]

        def load_chunk(i):
            nc.sync.dma_start(raw[i][:], wc_rows[:, :, load_starts[i] : load_starts[i] + LOADS[i]])

        xt_codes = keep.tile([P, T], U32, name="xt_codes", align_bytes=64)
        xs_codes = keep.tile([P, 2 * T], U8, name="xs_codes", align_bytes=64)
        ws_codes = keep.tile([P, J], U32, name="ws_codes", align_bytes=64)
        value_list = keep.tile([P, J // 16], U16, name="value_list")
        gate_list = keep.tile([P, J // 16], U16, name="gate_list")

        load_scale_rows(nc.gpsimd, xs_plane, xs_scales)
        load_chunk(0)
        nc.sync.dma_start(xt_codes[:].bitcast(I32), xt_words[0].rearrange("p n r -> p (n r)").bitcast(I32))
        load_scale_rows(nc.sync, xt_plane, xt_scales)
        load_chunk(1)
        load_chunk(2)
        load_chunk(3)
        nc.sync.dma_start(value_list[:], offs)
        nc.sync.dma_start(gate_list[:], offs2)
        nc.sync.dma_start(ws_codes[:].bitcast(I32), ws_words[0].rearrange("p n r -> p (n r)").bitcast(I32))
        nc.sync.dma_start(xs_codes[:].bitcast(I32), xs_words[0].bitcast(I32))
        load_scale_rows(nc.sync, ws_plane, ws_scales)

        z = [keep.tile([P, C], F32, name=f"z{m}") for m in range(TILES)]
        grouped = [keep.tile([P, w, PACK], BF16, name=f"grouped{i}", align_bytes=64) for i, w in enumerate(CHUNKS)]
        wc_codes = [keep.tile([P, w], U32, name=f"wc_codes{i}", align_bytes=64) for i, w in enumerate(CHUNKS)]
        wc_planes = [keep.tile([P, w], U8, name=f"wc_plane{i}", align_bytes=64) for i, w in enumerate(CHUNKS)]

        def interleave(i, copy):
            first = starts[i] - load_starts[LOAD_OF[i]]
            copy(
                grouped[i][:].rearrange("p (c i) r -> p c r i", i=4),
                raw[LOAD_OF[i]][:, :, first : first + CHUNKS[i]].rearrange("p r (c i) -> p c r i", i=4),
            )

        def quantise(i):
            nc.vector.quantize_mx(out=wc_codes[i][:].bitcast(FP8X4), scales=wc_planes[i][:], in_=grouped[i][:].rearrange("p c r -> p (c r)"))

        def z_product(i, m, bank_cols):
            cols = slice(m * P, (m + 1) * P)
            nc.tensor.matmul_mx(
                out=bank_cols, lhsT=xt_codes[:, cols].bitcast(FP8X4), lhsT_scale=xt_plane[:, cols],
                rhs=wc_codes[i][:].bitcast(FP8X4), rhs_scale=wc_planes[i][:], start=True, stop=True)

        def bank_tile(name, width, n):
            return psum.tile([P, width], F32, name=name, tag=f"bank{n}")

        def products(pieces, m, bank_cols):
            for i in pieces:
                first = starts[i] - starts[pieces[0]]
                z_product(i, m, bank_cols[:, first : first + CHUNKS[i]])

        def s_product(m, n):
            s_bank = bank_tile(f"sbank{m}", J, n)
            nc.tensor.matmul_mx(
                out=s_bank[:], lhsT=xs_codes[:, 2 * m * P : 2 * (m + 1) * P].bitcast(FP4X4), lhsT_scale=xs_plane[:, m * P : (m + 1) * P],
                rhs=ws_codes[:].bitcast(FP8X4), rhs_scale=ws_plane[:], start=True, stop=True)
            return s_bank

        def parts(*edges):
            return [(slice(a, b), slice(a // 16, b // 16)) for a, b in zip(edges, edges[1:])]

        whole, halves = parts(0, J), parts(0, J // 2, J)

        def pick(m, s_bank):
            gate = keep.tile([P, J], F32, name=f"gate{m}")
            factor = keep.tile([P, J], F32, name=f"factor{m}")
            result = keep.tile([P, J], F32, name=f"result{m}")
            rows = out[m * P : (m + 1) * P, :]
            for cols, entries in halves if m in (1, 2) else whole:
                nc.scalar.activation(gate[:, cols], z[m][:].indirect(gate_list[:, entries]), SIGMOID)
            if m == 0:
                value = keep.tile([P, J], F32, name="value")
                for cols, entries in halves:
                    nc.vector.tensor_copy(value[:, cols], z[m][:].indirect(value_list[:, entries]))
                for cols, entries in halves:
                    nc.vector.tensor_tensor(factor[:, cols], value[:, cols], s_bank[:, cols], MULT)
                for cols, entries in halves:
                    nc.vector.tensor_tensor(result[:, cols], factor[:, cols], gate[:, cols], MULT)
                nc.sync.dma_start(rows, result[:])
                return
            for cols, entries in halves:
                nc.vector.tensor_tensor(factor[:, cols], gate[:, cols], s_bank[:, cols], MULT)
            for cols, entries in halves if m < TILES - 1 else parts(0, J // 2, 3 * J // 4, J):
                nc.vector.tensor_tensor(result[:, cols], z[m][:].indirect(value_list[:, entries]), factor[:, cols], MULT)
                if m == TILES - 1:
                    nc.sync.dma_start(rows[:, cols], result[:, cols])
            if m < TILES - 1:
                nc.sync.dma_start(rows, result[:])

        for i in range(3):
            interleave(i, nc.vector.tensor_copy)
            quantise(i)
            for m in range(TILES):
                bank = bank_tile(f"zbank{i}_{m}", CHUNKS[i], (i % 2) * TILES + m)
                products((i,), m, bank[:])
                nc.scalar.copy(z[m][:, starts[i] : starts[i + 1]], bank[:])
        interleave(3, nc.vector.tensor_copy)
        interleave(4, nc.vector.tensor_copy)
        quantise(3)
        quantise(4)
        width = C - starts[3]
        for m, copy in ((0, nc.scalar.copy), (1, nc.vector.tensor_copy)):
            bank = bank_tile(f"zbank3_{m}", width, TILES + m)
            products((3, 4), m, bank[:])
            copy(z[m][:, starts[3] :], bank[:])
        for m in range(2):
            pick(m, s_product(m, m))
        bank = bank_tile("zbank3_late", 2 * width, 0)
        for m in range(2, TILES):
            products((3, 4), m, bank[:, (m - 2) * width : (m - 1) * width])
        for m in range(2, TILES):
            nc.scalar.copy(z[m][:, starts[3] :], bank[:, (m - 2) * width : (m - 1) * width])
        for m in range(2, TILES):
            pick(m, s_product(m, m))
